import numpy as np
import ml_dtypes


def mxq(x, axis, fmt="e4m3"):
    dtype, down = {"e4m3": (ml_dtypes.float8_e4m3fn, 7), "e5m2": (ml_dtypes.float8_e5m2, 14)}[fmt]
    v = np.moveaxis(np.asarray(x, np.float32).astype(ml_dtypes.bfloat16).astype(np.float64), axis, -1)
    blocks = v.reshape(v.shape[:-1] + (-1, 32))
    amax = np.abs(blocks).max(-1, keepdims=True)
    byte = np.maximum(np.where(amax > 0, np.frexp(amax)[1] - 1 + 127, 0) - down, 1)
    scale = np.exp2(byte - 127.0)
    codes = (blocks / scale).astype(np.float32).astype(dtype).astype(np.float64)
    return np.moveaxis((codes * scale).reshape(v.shape), -1, axis)


WIDE = False


def mx_kscale(k):
    if not WIDE:
        return np.ones(k)
    levels = np.array([10, -10, 5, -5, 0])
    if k % 512:
        return np.exp2(np.random.permutation(np.resize(levels, k // 32))).repeat(32)
    a = np.empty((k // 512, 16))
    for p in range(k // 512):
        a[p, :8] = np.random.permutation(np.resize(levels, 8))
        for g in range(8):
            far = levels[np.abs(levels - a[p, g]) >= 10]
            a[p, g + 8] = far[np.random.randint(len(far))]
    return np.exp2(a.ravel()).repeat(32)


def f64(x):
    return np.asarray(x).astype(np.float64)


def striped(idx):
    return np.tile(idx.reshape(-1, 16).T, (8, 1)).astype(np.uint16)


def unstriped(offs):
    return offs[:16].T.reshape(-1).astype(np.int64)


def pack_weight(w):
    k, n = w.shape
    w = f64(np.asarray(w, np.float32).astype(ml_dtypes.bfloat16)).reshape(k // 32, 32, n)
    amax = np.abs(w).max(1)
    byte = np.clip(np.where(amax > 0, np.frexp(amax)[1] - 1 + 127 - 7, 1), 1, 254)
    scaled = (w * np.exp2(127.0 - byte)[:, None, :]).reshape(k, n).astype(np.float32)
    words = np.ascontiguousarray(scaled.reshape(k // 512, 128, 4, n).transpose(0, 1, 3, 2)).astype(ml_dtypes.float8_e4m3fn).view(np.uint8)
    return words, np.ascontiguousarray(byte.astype(np.uint8).reshape(k // 512, 16, n))


def unpack_weight(words, scales):
    g, p, n, _ = words.shape
    vals = np.ascontiguousarray(words).view(ml_dtypes.float8_e4m3fn).astype(np.float64) * np.repeat(np.exp2(scales.astype(np.float64) - 127.0), 8, axis=1)[..., None]
    return vals.transpose(0, 1, 3, 2).reshape(g * 512, n)


def silu(v):
    return v / (1.0 + np.exp(-np.maximum(v, -700.0)))


K, T, S, H, Z, W = 512, 1024, 512, 512, 512, 2048
P = 2 ** 7


def setup_inputs():
    n = np.random.standard_normal
    s = mx_kscale(K)[:, None]
    u = mx_kscale(H)
    packed_xT = pack_weight(n((K, T)) * s)
    packed_eT = pack_weight(n((K, W)) * s)
    return {
        "x_words": packed_xT[0],
        "x_scales": packed_xT[1],
        "w1": (n((K, H)) / np.sqrt(K) / s).astype(np.float32),
        "w2": (n((K, H)) / np.sqrt(K) / s).astype(np.float32),
        "e_words": packed_eT[0],
        "e_scales": packed_eT[1],
        "w3": (n((K, H)) / np.sqrt(K) / s).astype(np.float32),
        "unit": (np.random.uniform(0.6, 1.4, (H, 1)) * u[:, None]).astype(np.float32),
        "unit2": (np.random.uniform(0.6, 1.4, (H, 1)) / np.sqrt(H) / u[:, None]).astype(np.float32),
        "frq": (np.tile(np.random.uniform(-0.5, 0.5, W), (P, 1))).astype(np.float32),
        "offs": striped(np.random.permutation(T)[:S]),
        "obj": striped(np.random.permutation(W)[:Z]),
        "ctx1": striped(np.random.permutation(S)),
    }


def reference(x_words, x_scales, w1, w2, e_words, e_scales, w3, unit, unit2, frq, offs, obj, ctx1):
    xq = unpack_weight(x_words, x_scales)[:, unstriped(offs)]
    y = mxq(f64(w1), 0, "e4m3").T @ xq
    yr = mxq(f64(w2), 0, "e4m3").T @ xq
    rc = yr[:, unstriped(ctx1)]
    sub_ = y * (np.tanh(rc) + 1.0)
    hid = f64(unit) * sub_
    e_obj = unpack_weight(e_words, e_scales)[:, unstriped(obj)]
    ye = mxq(f64(w3), 0, "e4m3").T @ e_obj
    obj_ = silu(ye)
    hid2 = f64(unit2) * obj_
    sc = mxq(hid, 0, "e4m3").T @ mxq(hid2, 0, "e4m3")
    best4 = sc.reshape(len(sc), -1, 4).max(axis=2)
    dev = sc - np.repeat(best4, 4, axis=1)
    return dev + f64(frq)[:1][:, unstriped(obj)]

@@ -1,0 +1,201 @@
+from contextlib import ExitStack
+
+import concourse.mybir as mybir
+
+F32 = mybir.dt.float32
+BF16 = mybir.dt.bfloat16
+I32 = mybir.dt.int32
+U32 = mybir.dt.uint32
+U16 = mybir.dt.uint16
+U8 = mybir.dt.uint8
+FP8X4 = mybir.dt.float8_e4m3fn_x4
+ALU = mybir.AluOpType
+ACT = mybir.ActivationFunctionType
+
+P = 128
+PACK = 4
+K = 512
+N = 512
+T_COLS = 1024
+W_COLS = 2048
+HALF = 256
+CH = 128
+FLOPS = 4 * 2 * 512 * 512 * 512
+
+
+def tile_picked_yscnrel_bias_p_kernel(tc, x_words, x_scales, w1, w2, e_words, e_scales, w3, unit, unit2, frq, offs, obj, ctx1, out):
+    nc = tc.nc
+    with ExitStack() as ctx:
+        sb = ctx.enter_context(tc.tile_pool(name="sb", bufs=1))
+        ps = ctx.enter_context(tc.psum_pool(name="ps", bufs=4))
+
+        def sbuf(shape, dtype, name):
+            return sb.tile(shape, dtype, name=name, align_bytes=64)
+
+        def load_list(src, name):
+            lst = sb.tile([P, N // 16], U16, name=name)
+            nc.sync.dma_start(lst[:], src)
+            return lst
+
+        def load_weight_half(w, h, name):
+            raw = sbuf([P, PACK, HALF], F32, name)
+            nc.sync.dma_start(raw[:], w[:, h * HALF : (h + 1) * HALF].rearrange("(p j) c -> p j c", j=PACK))
+            return raw
+
+        def load_words(words, cols, name):
+            table = sbuf([P, cols], U32, name)
+            nc.sync.dma_start(table[:].bitcast(I32), words[0].rearrange("p n t -> p (n t)").bitcast(I32))
+            return table
+
+        def load_scales(scales, cols, name, clear, queue):
+            table = sbuf([P, cols], U8, name)
+            clear.memset(table[:].bitcast(I32), 0)
+            for q in range(4):
+                queue.dma_start(table[32 * q : 32 * q + 4, :].bitcast(I32), scales[0, 4 * q : 4 * q + 4, :].bitcast(I32))
+            return table
+
+        def load_unit(src, name):
+            col = sbuf([P, PACK], F32, name)
+            nc.sync.dma_start(col[:], src.rearrange("(p t) o -> p (t o)", t=PACK))
+            return col
+
+        def cast_half(engine_copy, grouped, raw, h):
+            dst = grouped[:].rearrange("p (t m j) -> p m j t", t=PACK, j=PACK)[:, 64 * h : 64 * (h + 1)]
+            engine_copy(dst, raw[:].rearrange("p j (m t) -> p m j t", t=PACK))
+
+        def quantize(grouped_ap, codes_ap, scales_ap):
+            nc.vector.quantize_mx(out=codes_ap.bitcast(FP8X4), scales=scales_ap, in_=grouped_ap)
+
+        def mx(bank_ap, lhs, lcols, rhs, rcols):
+            nc.tensor.matmul_mx(out=bank_ap, lhsT=lhs[0][:, lcols].bitcast(FP8X4), lhsT_scale=lhs[1][:, lcols],
+                                rhs=rhs[0][:, rcols].bitcast(FP8X4), rhs_scale=rhs[1][:, rcols], start=True, stop=True)
+
+        def operand(name, cols):
+            return sbuf([P, cols], U32, name + "_codes"), sbuf([P, cols], U8, name + "_scales")
+
+        def blk(i, width=CH):
+            return slice(i * width, (i + 1) * width)
+
+        offs_t = load_list(offs, "offs_t")
+        xs_tab = load_scales(x_scales, T_COLS, "xs_tab", nc.vector, nc.sync)
+        xw_tab = load_words(x_words, T_COLS, "xw_tab")
+        w2_raw = [load_weight_half(w2, 0, "w2_raw0")]
+        obj_t = load_list(obj, "obj_t")
+        es_tab = load_scales(e_scales, W_COLS, "es_tab", nc.gpsimd, nc.sync)
+        w2_raw.append(load_weight_half(w2, 1, "w2_raw1"))
+        w3_raw = [load_weight_half(w3, 0, "w3_raw0")]
+        u1 = load_unit(unit, "u1")
+        w3_raw.append(load_weight_half(w3, 1, "w3_raw1"))
+        u2 = load_unit(unit2, "u2")
+        ew_tab = load_words(e_words, W_COLS, "ew_tab")
+        ctx_t = load_list(ctx1, "ctx_t")
+        w1_raw = [load_weight_half(w1, h, "w1_raw%d" % h) for h in range(2)]
+        frq_tab = sbuf([P, W_COLS], F32, "frq_tab")
+        nc.sync.dma_start(frq_tab[:], frq)
+
+        xq = operand("xq", N)
+        eq = operand("eq", N)
+        w1q, w2q, w3q = operand("w1q", N), operand("w2q", N), operand("w3q", N)
+        w1g, w2g, w3g = [sbuf([P, PACK * N], BF16, "w%dg" % i) for i in (1, 2, 3)]
+
+        nc.vector.tensor_copy(xq[1][:], xs_tab[:].indirect(offs_t[:]))
+        nc.vector.tensor_copy(xq[0][:], xw_tab[:].indirect(offs_t[:]))
+        nc.vector.tensor_copy(eq[1][:], es_tab[:].indirect(obj_t[:]))
+        cast_half(nc.scalar.copy, w2g, w2_raw[0], 0)
+        cast_half(nc.vector.tensor_copy, w2g, w2_raw[1], 1)
+        quantize(w2g[:], w2q[0][:], w2q[1][:])
+        cast_half(nc.scalar.copy, w3g, w3_raw[0], 0)
+        gate = []
+        for t in range(PACK):
+            bank = ps.tile([P, N], F32, name="bank_a")
+            mx(bank[:], w2q, blk(t), xq, slice(0, N))
+            th = sbuf([P, N], F32, "th%d" % t)
+            nc.scalar.activation(th[:], bank[:], ACT.Tanh)
+            win = sbuf([P, N], F32, "gate%d" % t)
+            nc.gpsimd.tensor_scalar(win[:], th[:], u1[:, t : t + 1], u1[:, t : t + 1], ALU.mult, ALU.add)
+            gate.append(win)
+
+        cast_half(nc.vector.tensor_copy, w3g, w3_raw[1], 1)
+        quantize(w3g[:], w3q[0][:], w3q[1][:])
+        for h in range(2):
+            nc.vector.tensor_copy(eq[0][:, blk(h, HALF)], ew_tab[:].indirect(obj_t[:, blk(h, 16)]))
+        h2q = operand("h2q", N)
+        h2g = []
+        for c in range(4):
+            bank = ps.tile([P, N], F32, name="bank_b")
+            for t in range(PACK):
+                mx(bank[:, blk(t)], w3q, blk(t), eq, blk(c))
+            sil = sbuf([P, CH, PACK], F32, "sil%d" % c)
+            nc.scalar.activation(sil[:], bank[:].rearrange("p (t e) -> p e t", t=PACK), ACT.Silu)
+            grouped = sbuf([P, CH, PACK], BF16, "h2g%d" % c)
+            nc.vector.tensor_tensor(grouped[:], sil[:], u2[:].unsqueeze(1).to_broadcast([P, CH, PACK]), ALU.mult)
+            h2g.append(grouped)
+            if c > 0:
+                quantize(h2g[c - 1][:].rearrange("p e t -> p (e t)"), h2q[0][:, blk(c - 1)], h2q[1][:, blk(c - 1)])
+        for h in range(2):
+            cast_half(nc.vector.tensor_copy, w1g, w1_raw[h], h)
+        quantize(h2g[3][:].rearrange("p e t -> p (e t)"), h2q[0][:, blk(3)], h2q[1][:, blk(3)])
+        quantize(w1g[:], w1q[0][:], w1q[1][:])
+
+        picked = []
+        for h in range(2):
+            g = sbuf([P, PACK, HALF], F32, "picked%d" % h)
+            for t in range(PACK):
+                nc.scalar.activation(g[:, t, :], gate[t][:].indirect(ctx_t[:, blk(h, 16)]), ACT.Copy)
+            picked.append(g)
+            if h == 0:
+                frq_picked = sbuf([P, N], F32, "frq_picked")
+                nc.scalar.activation(frq_picked[:], frq_tab[:].indirect(obj_t[:]), ACT.Copy)
+
+        y_banks = []
+        for c in range(4):
+            bank = ps.tile([P, N], F32, name="bank_a")
+            for t in range(PACK):
+                mx(bank[:, blk(t)], w1q, blk(t), xq, blk(c))
+            y_banks.append(bank)
+
+        hg, hq, sc, best = {}, {}, {}, {}
+
+        def hid_product(c):
+            hg[c] = sbuf([P, CH * PACK], BF16, "hg%d" % c)
+            nc.vector.tensor_tensor(
+                hg[c][:].rearrange("p (a i t) -> p a t i", i=4, t=PACK),
+                y_banks[c][:].rearrange("p (t a i) -> p a t i", i=4, t=PACK),
+                picked[c // 2][:, :, blk(c % 2)].rearrange("p t (a i) -> p a t i", i=4),
+                ALU.mult)
+
+        def hid_quantize(c):
+            hq[c] = operand("hq%d" % c, CH)
+            quantize(hg[c][:], hq[c][0][:], hq[c][1][:])
+            sc[c] = ps.tile([P, N], F32, name="bank_b")
+            mx(sc[c][:], hq[c], slice(0, CH), h2q, slice(0, N))
+
+        def best_of_four(c):
+            best[c] = sbuf([P, N // 4], F32, "best%d" % c)
+            nc.vector.tensor_reduce(best[c][:], sc[c][:].rearrange("p (z d) -> p z d", d=4), mybir.AxisListType.X, ALU.max)
+
+        def finish(c):
+            dev = sbuf([P, N // 4, 4], F32, "dev%d" % c)
+            nc.vector.tensor_tensor(dev[:], sc[c][:].rearrange("p (z d) -> p z d", d=4),
+                                    best[c][:].unsqueeze(2).to_broadcast([P, N // 4, 4]), ALU.subtract)
+            res = sbuf([P, N], F32, "res%d" % c)
+            adder = nc.vector if c == 3 else nc.gpsimd
+            adder.tensor_tensor(res[:], dev[:].rearrange("p z d -> p (z d)"), frq_picked[:], ALU.add)
+            nc.sync.dma_start(out[blk(c), :], res[:])
+
+        hid_product(0)
+        hid_product(1)
+        hid_quantize(0)
+        hid_quantize(1)
+        best_of_four(0)
+        hid_product(2)
+        finish(0)
+        hid_quantize(2)
+        best_of_four(1)
+        hid_product(3)
+        finish(1)
+        hid_quantize(3)
+        best_of_four(2)
+        best_of_four(3)
+        finish(2)
+        finish(3)

@@ -14,188 +14,247 @@ ACT = mybir.ActivationFunctionType
 
 P = 128
 PACK = 4
-K = 512
 N = 512
-T_COLS = 1024
-W_COLS = 2048
-HALF = 256
-CH = 128
-FLOPS = 4 * 2 * 512 * 512 * 512
+HALF = N // 2
+BLOCK = 128
+GROUP = 4
+X_COLS = 1024
+E_COLS = 2048
+LIST_ROWS = 16
+QUADRANT = 32
+FLOPS = 4 * 2 * N * N * N
 
 
-def tile_picked_yscnrel_bias_p_kernel(tc, x_words, x_scales, w1, w2, e_words, e_scales, w3, unit, unit2, frq, offs, obj, ctx1, out):
+def tile_picked_yscnrel_bias_p_kernel(
+    tc, x_words, x_scales, w1, w2, e_words, e_scales, w3, unit, unit2, frq, offs, obj, ctx1, out
+):
     nc = tc.nc
-    with ExitStack() as ctx:
-        sb = ctx.enter_context(tc.tile_pool(name="sb", bufs=1))
-        ps = ctx.enter_context(tc.psum_pool(name="ps", bufs=4))
+    with ExitStack() as stack:
+        sb = stack.enter_context(tc.tile_pool(name="sb", bufs=1))
+        ps = stack.enter_context(tc.psum_pool(name="ps", bufs=4))
 
-        def sbuf(shape, dtype, name):
-            return sb.tile(shape, dtype, name=name, align_bytes=64)
+        def sbuf(shape, dtype, name, reuse=None):
+            return sb.tile(shape, dtype, name=name, tag=reuse or name, align_bytes=64)
+
+        def part(index, width):
+            return slice(index * width, (index + 1) * width)
+
+        def mx_operand(name, cols):
+            return sbuf([P, cols], U32, name + "_words"), sbuf([P, cols], U8, name + "_scales")
 
         def load_list(src, name):
-            lst = sb.tile([P, N // 16], U16, name=name)
-            nc.sync.dma_start(lst[:], src)
-            return lst
+            entries = sb.tile([P, N // LIST_ROWS], U16, name=name)
+            nc.sync.dma_start(entries[:], src)
+            return entries
 
-        def load_weight_half(w, h, name):
+        def load_weight_half(w, half, name):
             raw = sbuf([P, PACK, HALF], F32, name)
-            nc.sync.dma_start(raw[:], w[:, h * HALF : (h + 1) * HALF].rearrange("(p j) c -> p j c", j=PACK))
+            nc.sync.dma_start(raw[:], w[:, part(half, HALF)].rearrange("(p j) c -> p j c", j=PACK))
             return raw
 
         def load_words(words, cols, name):
             table = sbuf([P, cols], U32, name)
-            nc.sync.dma_start(table[:].bitcast(I32), words[0].rearrange("p n t -> p (n t)").bitcast(I32))
+            src = words[0].rearrange("p n j -> p (n j)").bitcast(I32)
+            for piece in range(cols // X_COLS):
+                nc.sync.dma_start(table[:, part(piece, X_COLS)].bitcast(I32), src[:, part(piece, X_COLS)])
             return table
 
-        def load_scales(scales, cols, name, clear, queue):
+        def load_scale_rows(scales, cols, name, clearing_engine):
             table = sbuf([P, cols], U8, name)
-            clear.memset(table[:].bitcast(I32), 0)
-            for q in range(4):
-                queue.dma_start(table[32 * q : 32 * q + 4, :].bitcast(I32), scales[0, 4 * q : 4 * q + 4, :].bitcast(I32))
+            clearing_engine.memset(table[:].bitcast(I32), 0)
+            for r in range(PACK):
+                nc.sync.dma_start(table[r:P:QUADRANT, :].bitcast(I32), scales[0, r : PACK * PACK : PACK, :].bitcast(I32))
             return table
 
-        def load_unit(src, name):
-            col = sbuf([P, PACK], F32, name)
-            nc.sync.dma_start(col[:], src.rearrange("(p t) o -> p (t o)", t=PACK))
-            return col
+        def load_factors(src, name):
+            factors = sbuf([P, PACK], F32, name)
+            nc.sync.dma_start(factors[:], src.rearrange("(p t) o -> p (t o)", t=PACK))
+            return factors
 
-        def cast_half(engine_copy, grouped, raw, h):
-            dst = grouped[:].rearrange("p (t m j) -> p m j t", t=PACK, j=PACK)[:, 64 * h : 64 * (h + 1)]
-            engine_copy(dst, raw[:].rearrange("p j (m t) -> p m j t", t=PACK))
-
-        def quantize(grouped_ap, codes_ap, scales_ap):
-            nc.vector.quantize_mx(out=codes_ap.bitcast(FP8X4), scales=scales_ap, in_=grouped_ap)
-
-        def mx(bank_ap, lhs, lcols, rhs, rcols):
-            nc.tensor.matmul_mx(out=bank_ap, lhsT=lhs[0][:, lcols].bitcast(FP8X4), lhsT_scale=lhs[1][:, lcols],
-                                rhs=rhs[0][:, rcols].bitcast(FP8X4), rhs_scale=rhs[1][:, rcols], start=True, stop=True)
-
-        def operand(name, cols):
-            return sbuf([P, cols], U32, name + "_codes"), sbuf([P, cols], U8, name + "_scales")
-
-        def blk(i, width=CH):
-            return slice(i * width, (i + 1) * width)
-
-        offs_t = load_list(offs, "offs_t")
-        xs_tab = load_scales(x_scales, T_COLS, "xs_tab", nc.vector, nc.sync)
-        xw_tab = load_words(x_words, T_COLS, "xw_tab")
         w2_raw = [load_weight_half(w2, 0, "w2_raw0")]
-        obj_t = load_list(obj, "obj_t")
-        es_tab = load_scales(e_scales, W_COLS, "es_tab", nc.gpsimd, nc.sync)
+        offs_list = load_list(offs, "offs_list")
+        x_scale_table = load_scale_rows(x_scales, X_COLS, "x_scale_table", nc.vector)
         w2_raw.append(load_weight_half(w2, 1, "w2_raw1"))
+        x_word_table = load_words(x_words, X_COLS, "x_word_table")
+        obj_list = load_list(obj, "obj_list")
         w3_raw = [load_weight_half(w3, 0, "w3_raw0")]
-        u1 = load_unit(unit, "u1")
+        e_scale_table = load_scale_rows(e_scales, E_COLS, "e_scale_table", nc.gpsimd)
         w3_raw.append(load_weight_half(w3, 1, "w3_raw1"))
-        u2 = load_unit(unit2, "u2")
-        ew_tab = load_words(e_words, W_COLS, "ew_tab")
-        ctx_t = load_list(ctx1, "ctx_t")
-        w1_raw = [load_weight_half(w1, h, "w1_raw%d" % h) for h in range(2)]
-        frq_tab = sbuf([P, W_COLS], F32, "frq_tab")
-        nc.sync.dma_start(frq_tab[:], frq)
+        e_word_table = load_words(e_words, E_COLS, "e_word_table")
+        unit_cols = load_factors(unit, "unit_cols")
+        w1_raw = [load_weight_half(w1, half, "w1_raw%d" % half) for half in range(2)]
+        ctx_list = load_list(ctx1, "ctx_list")
+        unit2_cols = load_factors(unit2, "unit2_cols")
+        frq_table = sbuf([P, E_COLS], F32, "frq_table")
+        nc.sync.dma_start(frq_table[:], frq)
 
-        xq = operand("xq", N)
-        eq = operand("eq", N)
-        w1q, w2q, w3q = operand("w1q", N), operand("w2q", N), operand("w3q", N)
-        w1g, w2g, w3g = [sbuf([P, PACK * N], BF16, "w%dg" % i) for i in (1, 2, 3)]
+        warm_in = sbuf([P, 1], F32, "warm_in")
+        warm_out = sbuf([P, 1], F32, "warm_out")
+        nc.vector.memset(warm_in[:], 0.0)
+        nc.scalar.activation(warm_out[:], warm_in[:], ACT.Silu)
 
-        nc.vector.tensor_copy(xq[1][:], xs_tab[:].indirect(offs_t[:]))
-        nc.vector.tensor_copy(xq[0][:], xw_tab[:].indirect(offs_t[:]))
-        nc.vector.tensor_copy(eq[1][:], es_tab[:].indirect(obj_t[:]))
-        cast_half(nc.scalar.copy, w2g, w2_raw[0], 0)
-        cast_half(nc.vector.tensor_copy, w2g, w2_raw[1], 1)
-        quantize(w2g[:], w2q[0][:], w2q[1][:])
-        cast_half(nc.scalar.copy, w3g, w3_raw[0], 0)
+        def cast_weight_half(copy, dealt, raw, half):
+            dst = dealt[:].rearrange("p (t m j) -> p m j t", t=PACK, j=PACK)[:, part(half, P // 2)]
+            copy(dst, raw[:].rearrange("p j (m t) -> p m j t", t=PACK))
+
+        def quantize(values, operand, cols):
+            nc.vector.quantize_mx(out=operand[0][:, cols].bitcast(FP8X4), scales=operand[1][:, cols], in_=values)
+
+        def matmul(dst, stationary, stationary_cols, moving, moving_cols):
+            nc.tensor.matmul_mx(
+                out=dst,
+                lhsT=stationary[0][:, stationary_cols].bitcast(FP8X4),
+                lhsT_scale=stationary[1][:, stationary_cols],
+                rhs=moving[0][:, moving_cols].bitcast(FP8X4),
+                rhs_scale=moving[1][:, moving_cols],
+                start=True,
+                stop=True,
+            )
+
+        def planes_of_block(weight, picked, block, ring):
+            bank = ps.tile([P, N], F32, name=ring)
+            for t in range(PACK):
+                matmul(bank[:, part(t, BLOCK)], weight, part(t, P), picked, part(block, BLOCK))
+            return bank
+
+        every = slice(0, N)
+        x_picked, e_picked = mx_operand("x_picked", N), mx_operand("e_picked", N)
+        w1_mx, w2_mx, w3_mx = mx_operand("w1_mx", N), mx_operand("w2_mx", N), mx_operand("w3_mx", N)
+        w1_dealt = sbuf([P, PACK * N], BF16, "w1_dealt")
+        w2_dealt = sbuf([P, PACK * N], BF16, "w2_dealt")
+        w3_dealt = sbuf([P, PACK * N], BF16, "w3_dealt")
+        hid2_mx = mx_operand("hid2_mx", N)
+
+        nc.vector.tensor_copy(x_picked[1][:], x_scale_table[:].indirect(offs_list[:]))
+        cast_weight_half(nc.scalar.copy, w2_dealt, w2_raw[0], 0)
+        cast_weight_half(nc.vector.tensor_copy, w2_dealt, w2_raw[1], 1)
+        quantize(w2_dealt[:], w2_mx, every)
+        nc.vector.tensor_copy(x_picked[0][:], x_word_table[:].indirect(offs_list[:]))
+        nc.vector.tensor_copy(e_picked[1][:], e_scale_table[:].indirect(obj_list[:]))
+        cast_weight_half(nc.scalar.copy, w3_dealt, w3_raw[0], 0)
+        cast_weight_half(nc.vector.tensor_copy, w3_dealt, w3_raw[1], 1)
+        quantize(w3_dealt[:], w3_mx, every)
+
+        tanh_yr = sbuf([P, PACK, N], F32, "tanh_yr", reuse="w3_raw0")
+        for t in range(PACK):
+            bank = ps.tile([P, N], F32, name="subject")
+            matmul(bank[:], w2_mx, part(t, P), x_picked, every)
+            nc.scalar.activation(tanh_yr[:, t, :], bank[:], ACT.Tanh)
+
+        for half in range(2):
+            entries = obj_list[:, part(half, HALF // LIST_ROWS)]
+            nc.vector.tensor_copy(e_picked[0][:, part(half, HALF)], e_word_table[:].indirect(entries))
+
         gate = []
         for t in range(PACK):
-            bank = ps.tile([P, N], F32, name="bank_a")
-            mx(bank[:], w2q, blk(t), xq, slice(0, N))
-            th = sbuf([P, N], F32, "th%d" % t)
-            nc.scalar.activation(th[:], bank[:], ACT.Tanh)
-            win = sbuf([P, N], F32, "gate%d" % t)
-            nc.gpsimd.tensor_scalar(win[:], th[:], u1[:, t : t + 1], u1[:, t : t + 1], ALU.mult, ALU.add)
-            gate.append(win)
+            window = sbuf([P, N], F32, "gate%d" % t)
+            factor = unit_cols[:, t : t + 1]
+            if t < PACK // 2:
+                nc.vector.tensor_scalar(window[:], tanh_yr[:, t, :], factor, factor, ALU.mult, ALU.add)
+            else:
+                nc.scalar.activation(window[:], tanh_yr[:, t, :], ACT.Identity, bias=factor, scale=factor)
+            gate.append(window)
 
-        cast_half(nc.vector.tensor_copy, w3g, w3_raw[1], 1)
-        quantize(w3g[:], w3q[0][:], w3q[1][:])
-        for h in range(2):
-            nc.vector.tensor_copy(eq[0][:, blk(h, HALF)], ew_tab[:].indirect(obj_t[:, blk(h, 16)]))
-        h2q = operand("h2q", N)
-        h2g = []
-        for c in range(4):
-            bank = ps.tile([P, N], F32, name="bank_b")
+        silu_ye = []
+        for block in range(N // BLOCK):
+            bank = planes_of_block(w3_mx, e_picked, block, "object")
+            values = sbuf([P, BLOCK, PACK], F32, "silu_ye%d" % block)
+            nc.scalar.activation(values[:], bank[:].rearrange("p (t c) -> p c t", t=PACK), ACT.Silu)
+            silu_ye.append(values)
+
+        for half in range(2):
+            cast_weight_half(nc.vector.tensor_copy, w1_dealt, w1_raw[half], half)
+        quantize(w1_dealt[:], w1_mx, every)
+
+        hid2 = [
+            sbuf([P, HALF * PACK], BF16, "hid2_0", reuse="w1_raw1"),
+            sbuf([P, HALF * PACK], BF16, "hid2_1", reuse="w1_dealt"),
+        ]
+
+        def make_hid2(block):
+            dst = hid2[block // 2][:, part(block % 2, BLOCK * PACK)].rearrange("p (c t) -> p c t", t=PACK)
+            factors = unit2_cols[:].unsqueeze(1).to_broadcast([P, BLOCK, PACK])
+            nc.vector.tensor_tensor(dst, silu_ye[block][:], factors, ALU.mult)
+
+        def quantize_hid2(half):
+            quantize(hid2[half][:], hid2_mx, part(half, HALF))
+
+        def gather_gates(half):
+            picked = sbuf([P, PACK, HALF], F32, "gate_picked%d" % half)
+            entries = ctx_list[:, part(half, HALF // LIST_ROWS)]
             for t in range(PACK):
-                mx(bank[:, blk(t)], w3q, blk(t), eq, blk(c))
-            sil = sbuf([P, CH, PACK], F32, "sil%d" % c)
-            nc.scalar.activation(sil[:], bank[:].rearrange("p (t e) -> p e t", t=PACK), ACT.Silu)
-            grouped = sbuf([P, CH, PACK], BF16, "h2g%d" % c)
-            nc.vector.tensor_tensor(grouped[:], sil[:], u2[:].unsqueeze(1).to_broadcast([P, CH, PACK]), ALU.mult)
-            h2g.append(grouped)
-            if c > 0:
-                quantize(h2g[c - 1][:].rearrange("p e t -> p (e t)"), h2q[0][:, blk(c - 1)], h2q[1][:, blk(c - 1)])
-        for h in range(2):
-            cast_half(nc.vector.tensor_copy, w1g, w1_raw[h], h)
-        quantize(h2g[3][:].rearrange("p e t -> p (e t)"), h2q[0][:, blk(3)], h2q[1][:, blk(3)])
-        quantize(w1g[:], w1q[0][:], w1q[1][:])
+                nc.scalar.activation(picked[:, t, :], gate[t][:].indirect(entries), ACT.Copy)
+            return picked
 
-        picked = []
-        for h in range(2):
-            g = sbuf([P, PACK, HALF], F32, "picked%d" % h)
-            for t in range(PACK):
-                nc.scalar.activation(g[:, t, :], gate[t][:].indirect(ctx_t[:, blk(h, 16)]), ACT.Copy)
-            picked.append(g)
-            if h == 0:
-                frq_picked = sbuf([P, N], F32, "frq_picked")
-                nc.scalar.activation(frq_picked[:], frq_tab[:].indirect(obj_t[:]), ACT.Copy)
+        make_hid2(0)
+        make_hid2(1)
+        y_banks = [planes_of_block(w1_mx, x_picked, block, "subject") for block in range(N // BLOCK)]
+        gate_picked = [gather_gates(0)]
+        make_hid2(2)
+        quantize_hid2(0)
+        make_hid2(3)
+        gate_picked.append(gather_gates(1))
+        frq_picked = sbuf([P, N], F32, "frq_picked", reuse="silu_ye3")
+        nc.scalar.activation(frq_picked[:], frq_table[:].indirect(obj_list[:]), ACT.Copy)
+        quantize_hid2(1)
 
-        y_banks = []
-        for c in range(4):
-            bank = ps.tile([P, N], F32, name="bank_a")
-            for t in range(PACK):
-                mx(bank[:, blk(t)], w1q, blk(t), xq, blk(c))
-            y_banks.append(bank)
+        hid, hid_mx, scores, best, dev = {}, {}, {}, {}, {}
 
-        hg, hq, sc, best = {}, {}, {}, {}
-
-        def hid_product(c):
-            hg[c] = sbuf([P, CH * PACK], BF16, "hg%d" % c)
+        def make_hid(block):
+            if block % 2 == 0:
+                hid[block // 2] = sbuf([P, HALF * PACK], BF16, "hid%d" % (block // 2), reuse="hid0")
             nc.vector.tensor_tensor(
-                hg[c][:].rearrange("p (a i t) -> p a t i", i=4, t=PACK),
-                y_banks[c][:].rearrange("p (t a i) -> p a t i", i=4, t=PACK),
-                picked[c // 2][:, :, blk(c % 2)].rearrange("p t (a i) -> p a t i", i=4),
-                ALU.mult)
+                hid[block // 2][:, part(block % 2, BLOCK * PACK)].rearrange("p (a c t) -> p a t c", c=4, t=PACK),
+                y_banks[block][:].rearrange("p (t a c) -> p a t c", c=4, t=PACK),
+                gate_picked[block // 2][:, :, part(block % 2, BLOCK)].rearrange("p t (a c) -> p a t c", c=4),
+                ALU.mult,
+            )
 
-        def hid_quantize(c):
-            hq[c] = operand("hq%d" % c, CH)
-            quantize(hg[c][:], hq[c][0][:], hq[c][1][:])
-            sc[c] = ps.tile([P, N], F32, name="bank_b")
-            mx(sc[c][:], hq[c], slice(0, CH), h2q, slice(0, N))
+        def quantize_hid(half):
+            hid_mx[half] = mx_operand("hid_mx%d" % half, HALF)
+            quantize(hid[half][:], hid_mx[half], slice(0, HALF))
 
-        def best_of_four(c):
-            best[c] = sbuf([P, N // 4], F32, "best%d" % c)
-            nc.vector.tensor_reduce(best[c][:], sc[c][:].rearrange("p (z d) -> p z d", d=4), mybir.AxisListType.X, ALU.max)
+        def make_scores(half):
+            for block in (2 * half, 2 * half + 1):
+                bank = ps.tile([P, N], F32, name="object")
+                matmul(bank[:], hid_mx[half], part(block % 2, BLOCK), hid2_mx, every)
+                scores[block] = bank[:].rearrange("p (z d) -> p z d", d=GROUP)
 
-        def finish(c):
-            dev = sbuf([P, N // 4, 4], F32, "dev%d" % c)
-            nc.vector.tensor_tensor(dev[:], sc[c][:].rearrange("p (z d) -> p z d", d=4),
-                                    best[c][:].unsqueeze(2).to_broadcast([P, N // 4, 4]), ALU.subtract)
-            res = sbuf([P, N], F32, "res%d" % c)
-            adder = nc.vector if c == 3 else nc.gpsimd
-            adder.tensor_tensor(res[:], dev[:].rearrange("p z d -> p (z d)"), frq_picked[:], ALU.add)
-            nc.sync.dma_start(out[blk(c), :], res[:])
+        def best_of_group(block, reuse=None):
+            best[block] = sbuf([P, N // GROUP], F32, "best%d" % block, reuse=reuse)
+            nc.vector.tensor_reduce(best[block][:], scores[block], mybir.AxisListType.X, ALU.max)
 
-        hid_product(0)
-        hid_product(1)
-        hid_quantize(0)
-        hid_quantize(1)
-        best_of_four(0)
-        hid_product(2)
-        finish(0)
-        hid_quantize(2)
-        best_of_four(1)
-        hid_product(3)
-        finish(1)
-        hid_quantize(3)
-        best_of_four(2)
-        best_of_four(3)
-        finish(2)
-        finish(3)
+        def subtract_best(block, piece=0, pieces=1):
+            groups = N // GROUP // pieces
+            dev[block, piece] = sbuf([P, groups, GROUP], F32, "dev%d_%d" % (block, piece))
+            largest = best[block][:, part(piece, groups)].unsqueeze(2).to_broadcast([P, groups, GROUP])
+            nc.vector.tensor_tensor(dev[block, piece][:], scores[block][:, part(piece, groups), :], largest, ALU.subtract)
+
+        def add_frq_and_store(engine, block, piece=0, pieces=1):
+            cols = part(piece, N // pieces)
+            result = sbuf([P, N // pieces], F32, "result%d_%d" % (block, piece))
+            engine.tensor_tensor(result[:], dev[block, piece][:].rearrange("p z d -> p (z d)"), frq_picked[:, cols], ALU.add)
+            nc.sync.dma_start(out[part(block, BLOCK), cols], result[:])
+
+        make_hid(0)
+        make_hid(1)
+        quantize_hid(0)
+        make_scores(0)
+        make_hid(2)
+        best_of_group(0)
+        make_hid(3)
+        subtract_best(0)
+        quantize_hid(1)
+        add_frq_and_store(nc.gpsimd, 0)
+        make_scores(1)
+        best_of_group(1, reuse="best0")
+        subtract_best(1)
+        add_frq_and_store(nc.gpsimd, 1)
+        best_of_group(2)
+        best_of_group(3)
+        subtract_best(2)
+        add_frq_and_store(nc.vector, 2)
+        for piece in range(2):
+            subtract_best(3, piece, 2)
+        for piece in range(2):
+            add_frq_and_store(nc.vector, 3, piece, 2)

from contextlib import ExitStack

import concourse.mybir as mybir

F32 = mybir.dt.float32
BF16 = mybir.dt.bfloat16
I32 = mybir.dt.int32
U32 = mybir.dt.uint32
U16 = mybir.dt.uint16
U8 = mybir.dt.uint8
FP8X4 = mybir.dt.float8_e4m3fn_x4
ALU = mybir.AluOpType
ACT = mybir.ActivationFunctionType

P = 128
PACK = 4
N = 512
HALF = N // 2
BLOCK = 128
GROUP = 4
X_COLS = 1024
E_COLS = 2048
LIST_ROWS = 16
QUADRANT = 32
FLOPS = 4 * 2 * N * N * N


def tile_picked_yscnrel_bias_p_kernel(
    tc, x_words, x_scales, w1, w2, e_words, e_scales, w3, unit, unit2, frq, offs, obj, ctx1, out
):
    nc = tc.nc
    with ExitStack() as stack:
        sb = stack.enter_context(tc.tile_pool(name="sb", bufs=1))
        ps = stack.enter_context(tc.psum_pool(name="ps", bufs=4))

        def sbuf(shape, dtype, name, reuse=None):
            return sb.tile(shape, dtype, name=name, tag=reuse or name, align_bytes=64)

        def part(index, width):
            return slice(index * width, (index + 1) * width)

        def mx_operand(name, cols):
            return sbuf([P, cols], U32, name + "_words"), sbuf([P, cols], U8, name + "_scales")

        def load_list(src, name):
            entries = sb.tile([P, N // LIST_ROWS], U16, name=name)
            nc.sync.dma_start(entries[:], src)
            return entries

        def load_weight_half(w, half, name):
            raw = sbuf([P, PACK, HALF], F32, name)
            nc.sync.dma_start(raw[:], w[:, part(half, HALF)].rearrange("(p j) c -> p j c", j=PACK))
            return raw

        def load_words(words, cols, name):
            table = sbuf([P, cols], U32, name)
            src = words[0].rearrange("p n j -> p (n j)").bitcast(I32)
            for piece in range(cols // X_COLS):
                nc.sync.dma_start(table[:, part(piece, X_COLS)].bitcast(I32), src[:, part(piece, X_COLS)])
            return table

        def load_scale_rows(scales, cols, name, clearing_engine):
            table = sbuf([P, cols], U8, name)
            clearing_engine.memset(table[:].bitcast(I32), 0)
            for r in range(PACK):
                nc.sync.dma_start(table[r:P:QUADRANT, :].bitcast(I32), scales[0, r : PACK * PACK : PACK, :].bitcast(I32))
            return table

        def load_factors(src, name):
            factors = sbuf([P, PACK], F32, name)
            nc.sync.dma_start(factors[:], src.rearrange("(p t) o -> p (t o)", t=PACK))
            return factors

        w2_raw = [load_weight_half(w2, 0, "w2_raw0")]
        offs_list = load_list(offs, "offs_list")
        x_scale_table = load_scale_rows(x_scales, X_COLS, "x_scale_table", nc.vector)
        w2_raw.append(load_weight_half(w2, 1, "w2_raw1"))
        x_word_table = load_words(x_words, X_COLS, "x_word_table")
        obj_list = load_list(obj, "obj_list")
        w3_raw = [load_weight_half(w3, 0, "w3_raw0")]
        e_scale_table = load_scale_rows(e_scales, E_COLS, "e_scale_table", nc.gpsimd)
        w3_raw.append(load_weight_half(w3, 1, "w3_raw1"))
        e_word_table = load_words(e_words, E_COLS, "e_word_table")
        unit_cols = load_factors(unit, "unit_cols")
        w1_raw = [load_weight_half(w1, half, "w1_raw%d" % half) for half in range(2)]
        ctx_list = load_list(ctx1, "ctx_list")
        unit2_cols = load_factors(unit2, "unit2_cols")
        frq_table = sbuf([P, E_COLS], F32, "frq_table")
        nc.sync.dma_start(frq_table[:], frq)

        warm_in = sbuf([P, 1], F32, "warm_in")
        warm_out = sbuf([P, 1], F32, "warm_out")
        nc.vector.memset(warm_in[:], 0.0)
        nc.scalar.activation(warm_out[:], warm_in[:], ACT.Silu)

        def cast_weight_half(copy, dealt, raw, half):
            dst = dealt[:].rearrange("p (t m j) -> p m j t", t=PACK, j=PACK)[:, part(half, P // 2)]
            copy(dst, raw[:].rearrange("p j (m t) -> p m j t", t=PACK))

        def quantize(values, operand, cols):
            nc.vector.quantize_mx(out=operand[0][:, cols].bitcast(FP8X4), scales=operand[1][:, cols], in_=values)

        def matmul(dst, stationary, stationary_cols, moving, moving_cols):
            nc.tensor.matmul_mx(
                out=dst,
                lhsT=stationary[0][:, stationary_cols].bitcast(FP8X4),
                lhsT_scale=stationary[1][:, stationary_cols],
                rhs=moving[0][:, moving_cols].bitcast(FP8X4),
                rhs_scale=moving[1][:, moving_cols],
                start=True,
                stop=True,
            )

        def planes_of_block(weight, picked, block, ring):
            bank = ps.tile([P, N], F32, name=ring)
            for t in range(PACK):
                matmul(bank[:, part(t, BLOCK)], weight, part(t, P), picked, part(block, BLOCK))
            return bank

        every = slice(0, N)
        x_picked, e_picked = mx_operand("x_picked", N), mx_operand("e_picked", N)
        w1_mx, w2_mx, w3_mx = mx_operand("w1_mx", N), mx_operand("w2_mx", N), mx_operand("w3_mx", N)
        w1_dealt = sbuf([P, PACK * N], BF16, "w1_dealt")
        w2_dealt = sbuf([P, PACK * N], BF16, "w2_dealt")
        w3_dealt = sbuf([P, PACK * N], BF16, "w3_dealt")
        hid2_mx = mx_operand("hid2_mx", N)

        nc.vector.tensor_copy(x_picked[1][:], x_scale_table[:].indirect(offs_list[:]))
        cast_weight_half(nc.scalar.copy, w2_dealt, w2_raw[0], 0)
        cast_weight_half(nc.vector.tensor_copy, w2_dealt, w2_raw[1], 1)
        quantize(w2_dealt[:], w2_mx, every)
        nc.vector.tensor_copy(x_picked[0][:], x_word_table[:].indirect(offs_list[:]))
        nc.vector.tensor_copy(e_picked[1][:], e_scale_table[:].indirect(obj_list[:]))
        cast_weight_half(nc.scalar.copy, w3_dealt, w3_raw[0], 0)
        cast_weight_half(nc.vector.tensor_copy, w3_dealt, w3_raw[1], 1)
        quantize(w3_dealt[:], w3_mx, every)

        tanh_yr = sbuf([P, PACK, N], F32, "tanh_yr", reuse="w3_raw0")
        for t in range(PACK):
            bank = ps.tile([P, N], F32, name="subject")
            matmul(bank[:], w2_mx, part(t, P), x_picked, every)
            nc.scalar.activation(tanh_yr[:, t, :], bank[:], ACT.Tanh)

        for half in range(2):
            entries = obj_list[:, part(half, HALF // LIST_ROWS)]
            nc.vector.tensor_copy(e_picked[0][:, part(half, HALF)], e_word_table[:].indirect(entries))

        gate = []
        for t in range(PACK):
            window = sbuf([P, N], F32, "gate%d" % t)
            factor = unit_cols[:, t : t + 1]
            if t < PACK // 2:
                nc.vector.tensor_scalar(window[:], tanh_yr[:, t, :], factor, factor, ALU.mult, ALU.add)
            else:
                nc.scalar.activation(window[:], tanh_yr[:, t, :], ACT.Identity, bias=factor, scale=factor)
            gate.append(window)

        silu_ye = []
        for block in range(N // BLOCK):
            bank = planes_of_block(w3_mx, e_picked, block, "object")
            values = sbuf([P, BLOCK, PACK], F32, "silu_ye%d" % block)
            nc.scalar.activation(values[:], bank[:].rearrange("p (t c) -> p c t", t=PACK), ACT.Silu)
            silu_ye.append(values)

        for half in range(2):
            cast_weight_half(nc.vector.tensor_copy, w1_dealt, w1_raw[half], half)
        quantize(w1_dealt[:], w1_mx, every)

        hid2 = [
            sbuf([P, HALF * PACK], BF16, "hid2_0", reuse="w1_raw1"),
            sbuf([P, HALF * PACK], BF16, "hid2_1", reuse="w1_dealt"),
        ]

        def make_hid2(block):
            dst = hid2[block // 2][:, part(block % 2, BLOCK * PACK)].rearrange("p (c t) -> p c t", t=PACK)
            factors = unit2_cols[:].unsqueeze(1).to_broadcast([P, BLOCK, PACK])
            nc.vector.tensor_tensor(dst, silu_ye[block][:], factors, ALU.mult)

        def quantize_hid2(half):
            quantize(hid2[half][:], hid2_mx, part(half, HALF))

        def gather_gates(half):
            picked = sbuf([P, PACK, HALF], F32, "gate_picked%d" % half)
            entries = ctx_list[:, part(half, HALF // LIST_ROWS)]
            for t in range(PACK):
                nc.scalar.activation(picked[:, t, :], gate[t][:].indirect(entries), ACT.Copy)
            return picked

        make_hid2(0)
        make_hid2(1)
        y_banks = [planes_of_block(w1_mx, x_picked, block, "subject") for block in range(N // BLOCK)]
        gate_picked = [gather_gates(0)]
        make_hid2(2)
        quantize_hid2(0)
        make_hid2(3)
        gate_picked.append(gather_gates(1))
        frq_picked = sbuf([P, N], F32, "frq_picked", reuse="silu_ye3")
        nc.scalar.activation(frq_picked[:], frq_table[:].indirect(obj_list[:]), ACT.Copy)
        quantize_hid2(1)

        hid, hid_mx, scores, best, dev = {}, {}, {}, {}, {}

        def make_hid(block):
            if block % 2 == 0:
                hid[block // 2] = sbuf([P, HALF * PACK], BF16, "hid%d" % (block // 2), reuse="hid0")
            nc.vector.tensor_tensor(
                hid[block // 2][:, part(block % 2, BLOCK * PACK)].rearrange("p (a c t) -> p a t c", c=4, t=PACK),
                y_banks[block][:].rearrange("p (t a c) -> p a t c", c=4, t=PACK),
                gate_picked[block // 2][:, :, part(block % 2, BLOCK)].rearrange("p t (a c) -> p a t c", c=4),
                ALU.mult,
            )

        def quantize_hid(half):
            hid_mx[half] = mx_operand("hid_mx%d" % half, HALF)
            quantize(hid[half][:], hid_mx[half], slice(0, HALF))

        def make_scores(half):
            for block in (2 * half, 2 * half + 1):
                bank = ps.tile([P, N], F32, name="object")
                matmul(bank[:], hid_mx[half], part(block % 2, BLOCK), hid2_mx, every)
                scores[block] = bank[:].rearrange("p (z d) -> p z d", d=GROUP)

        def best_of_group(block, reuse=None):
            best[block] = sbuf([P, N // GROUP], F32, "best%d" % block, reuse=reuse)
            nc.vector.tensor_reduce(best[block][:], scores[block], mybir.AxisListType.X, ALU.max)

        def subtract_best(block, piece=0, pieces=1):
            groups = N // GROUP // pieces
            dev[block, piece] = sbuf([P, groups, GROUP], F32, "dev%d_%d" % (block, piece))
            largest = best[block][:, part(piece, groups)].unsqueeze(2).to_broadcast([P, groups, GROUP])
            nc.vector.tensor_tensor(dev[block, piece][:], scores[block][:, part(piece, groups), :], largest, ALU.subtract)

        def add_frq_and_store(engine, block, piece=0, pieces=1):
            cols = part(piece, N // pieces)
            result = sbuf([P, N // pieces], F32, "result%d_%d" % (block, piece))
            engine.tensor_tensor(result[:], dev[block, piece][:].rearrange("p z d -> p (z d)"), frq_picked[:, cols], ALU.add)
            nc.sync.dma_start(out[part(block, BLOCK), cols], result[:])

        make_hid(0)
        make_hid(1)
        quantize_hid(0)
        make_scores(0)
        make_hid(2)
        best_of_group(0)
        make_hid(3)
        subtract_best(0)
        quantize_hid(1)
        add_frq_and_store(nc.gpsimd, 0)
        make_scores(1)
        best_of_group(1, reuse="best0")
        subtract_best(1)
        add_frq_and_store(nc.gpsimd, 1)
        best_of_group(2)
        best_of_group(3)
        subtract_best(2)
        add_frq_and_store(nc.vector, 2)
        for piece in range(2):
            subtract_best(3, piece, 2)
        for piece in range(2):
            add_frq_and_store(nc.vector, 3, piece, 2)
